import numpy as np
import ml_dtypes


def mxq(x, axis, fmt="e4m3"):
    dtype, down = {"e4m3": (ml_dtypes.float8_e4m3fn, 7), "e5m2": (ml_dtypes.float8_e5m2, 14)}[fmt]
    v = np.moveaxis(np.asarray(x, np.float32).astype(ml_dtypes.bfloat16).astype(np.float64), axis, -1)
    blocks = v.reshape(v.shape[:-1] + (-1, 32))
    amax = np.abs(blocks).max(-1, keepdims=True)
    byte = np.maximum(np.where(amax > 0, np.frexp(amax)[1] - 1 + 127, 0) - down, 1)
    scale = np.exp2(byte - 127.0)
    codes = (blocks / scale).astype(np.float32).astype(dtype).astype(np.float64)
    return np.moveaxis((codes * scale).reshape(v.shape), -1, axis)


WIDE = False


def mx_kscale(k):
    if not WIDE:
        return np.ones(k)
    levels = np.array([10, -10, 5, -5, 0])
    if k % 512:
        return np.exp2(np.random.permutation(np.resize(levels, k // 32))).repeat(32)
    a = np.empty((k // 512, 16))
    for p in range(k // 512):
        a[p, :8] = np.random.permutation(np.resize(levels, 8))
        for g in range(8):
            far = levels[np.abs(levels - a[p, g]) >= 10]
            a[p, g + 8] = far[np.random.randint(len(far))]
    return np.exp2(a.ravel()).repeat(32)


BF16 = ml_dtypes.bfloat16


def bf(x):
    return np.asarray(x, np.float32).astype(BF16)


def f64(x):
    return np.asarray(x).astype(np.float64)


E2M1 = np.array([0.0, 0.5, 1.0, 1.5, 2.0, 3.0, 4.0, 6.0, -0.0, -0.5, -1.0, -1.5, -2.0, -3.0, -4.0, -6.0])


def pack_weight(w, fmt):
    k, n = w.shape
    w = f64(bf(w)).reshape(k // 32, 32, n)
    amax = np.abs(w).max(1)
    if fmt == "e4m3":
        byte = np.frexp(amax)[1] - 1 + 127 - 7
    else:
        mant, ex = np.frexp(amax / 6.0)
        byte = np.where(mant > 0.5, ex, ex - 1) + 127
    byte = np.clip(np.where(amax > 0, byte, 1), 1, 254)
    scaled = (w * np.exp2(127.0 - byte)[:, None, :]).reshape(k, n).astype(np.float32)
    by_word = np.ascontiguousarray(scaled.reshape(k // 512, 128, 4, n).transpose(0, 1, 3, 2))
    if fmt == "e4m3":
        words = by_word.astype(ml_dtypes.float8_e4m3fn).view(np.uint8)
    else:
        c = by_word.astype(ml_dtypes.float4_e2m1fn).view(np.uint8) & 0xF
        words = c[..., 0::2] | (c[..., 1::2] << 4)
    return np.ascontiguousarray(words), np.ascontiguousarray(byte.astype(np.uint8).reshape(k // 512, 16, n))


def unpack_weight(words, scales, fmt):
    g, p, n, _ = words.shape
    if fmt == "e4m3":
        vals = np.ascontiguousarray(words).view(ml_dtypes.float8_e4m3fn).astype(np.float64)
    else:
        nib = np.empty((g, p, n, 4), np.uint8)
        nib[..., 0::2] = words & 0xF
        nib[..., 1::2] = words >> 4
        vals = E2M1[nib]
    vals = vals * np.repeat(np.exp2(scales.astype(np.float64) - 127.0), 8, axis=1)[..., None]
    return vals.transpose(0, 1, 3, 2).reshape(g * 512, n)
def pack4(w):
    words, scales = pack_weight(w, "e2m1")
    return words.reshape(words.shape[0], 128, -1), scales


def unpack4(words, scales):
    return unpack_weight(words.reshape(words.shape[0], 128, -1, 2), scales, "e2m1")


N, D, P, G, H = 1024, 1024, 512, 512, 1024


def sigmoid(v):
    return 1.0 / (1.0 + np.exp(-v))


def draw0():
    s, u, t = mx_kscale(D), mx_kscale(P), mx_kscale(G)
    x = bf(np.random.standard_normal((N, D)) * s)
    prior = bf(np.random.standard_normal((N, P)) * u)
    wx_words, wx_scales = pack4(np.random.standard_normal((D, G)) / np.sqrt(D) / s[:, None] * t)
    wp_words, wp_scales = pack4(np.random.standard_normal((P, G)) / np.sqrt(P) / u[:, None] * t)
    b1 = bf(np.random.standard_normal(G) * 0.5 * t)
    w2_words, w2_scales = pack4(np.random.standard_normal((G, H)) / np.sqrt(G) / t[:, None])
    wl_words, wl_scales = pack4(np.random.standard_normal((D, H)) / np.sqrt(D) / s[:, None])
    return {
        "x": x,
        "prior": prior,
        "wx_words": wx_words,
        "wx_scales": wx_scales,
        "wp_words": wp_words,
        "wp_scales": wp_scales,
        "b1": b1,
        "w2_words": w2_words,
        "w2_scales": w2_scales,
        "wl_words": wl_words,
        "wl_scales": wl_scales,
    }


def core(x, prior, wx_words, wx_scales, wp_words, wp_scales, b1, w2_words, w2_scales, wl_words, wl_scales):
    xq = mxq(f64(x), 1, "e4m3")
    pq = mxq(f64(prior), 1, "e4m3")
    a = (pq @ unpack4(wp_words, wp_scales)) + (xq @ unpack4(wx_words, wx_scales)) + f64(b1)[None, :]
    r = np.maximum(a, 0.0)
    t = mxq(r, 1, "e4m3") @ unpack4(w2_words, w2_scales)
    gate = 2.0 * sigmoid(t)
    h = np.maximum(xq @ unpack4(wl_words, wl_scales), 0.0)
    return gate * h


def e4m3fn_bytes(y):
    return np.clip(np.asarray(y, np.float64), -448.0, 448.0).astype(np.float32).astype(ml_dtypes.float8_e4m3fn).view(np.uint8)


def e4m3fn_values(b):
    return np.asarray(b, np.uint8).view(ml_dtypes.float8_e4m3fn).astype(np.float64)


def setup_inputs():
    d = draw0()
    x0 = np.asarray(d['x']).astype(np.float64)
    s = (np.max(np.abs(x0), axis=(0,), keepdims=True) / 448.0).astype(np.float32)
    out = {}
    for k, v in d.items():
        if k == 'x':
            out['x_bytes'] = e4m3fn_bytes(x0 / s.astype(np.float64))
            out['x_scale'] = s
        else:
            out[k] = v
    return out


def reference(x_bytes, x_scale, prior, wx_words, wx_scales, wp_words, wp_scales, b1, w2_words, w2_scales, wl_words, wl_scales):
    return core(e4m3fn_values(x_bytes) * x_scale.astype(np.float64), prior, wx_words, wx_scales, wp_words, wp_scales, b1, w2_words, w2_scales, wl_words, wl_scales)

@@ -1,0 +1,297 @@
+from contextlib import ExitStack
+
+import concourse.mybir as mybir
+from concourse.masks import make_identity
+
+P = 128
+TOKENS, D, PRIOR, G, HID = 1024, 1024, 512, 512, 1024
+NT = TOKENS // P
+BANK = 512
+FLOPS = 2 * TOKENS * (D * G + PRIOR * G + G * HID + D * HID)
+
+F32 = mybir.dt.float32
+BF16 = mybir.dt.bfloat16
+I32 = mybir.dt.int32
+U32 = mybir.dt.uint32
+U8 = mybir.dt.uint8
+FP8 = mybir.dt.float8_e4m3fn
+FP8X4 = mybir.dt.float8_e4m3fn_x4
+FP4X4 = mybir.dt.float4_e2m1fn_x4
+ACT = mybir.ActivationFunctionType
+ALU = mybir.AluOpType
+
+
+def tile_pepnetpriorgatedhiddenlayer_w4_kernel(
+    tc, x_bytes, x_scale, prior, wx_words, wx_scales, wp_words, wp_scales, b1, w2_words, w2_scales, wl_words, wl_scales, out
+):
+    nc = tc.nc
+    with ExitStack() as ctx:
+        keep = ctx.enter_context(tc.tile_pool(name="keep", bufs=1))
+        work = ctx.enter_context(tc.tile_pool(name="work", bufs=3))
+        psum = ctx.enter_context(tc.psum_pool(name="psum", bufs=1))
+
+        dummy = keep.tile([P, 1], F32)
+        nc.vector.memset(dummy[:], 0.0)
+        nc.scalar.activation(out=dummy[:], in_=dummy[:], func=ACT.Sigmoid)
+        ident = keep.tile([P, P], F32)
+        make_identity(nc, ident[:])
+        ident_bf = keep.tile([P, P], BF16)
+        nc.gpsimd.tensor_copy(out=ident_bf[:], in_=ident[:])
+
+        a_scales = keep.tile([P, 3, G], U8, align_bytes=64)
+        w2_sc = keep.tile([P, HID], U8, align_bytes=64)
+        wl_sc = keep.tile([P, 2, HID], U8, align_bytes=64)
+        nc.vector.memset(a_scales[:].rearrange("p c n -> p (c n)").bitcast(I32), 0)
+        nc.vector.memset(w2_sc[:].bitcast(I32), 0)
+        nc.vector.memset(wl_sc[:].rearrange("p c n -> p (c n)").bitcast(I32), 0)
+
+        s_col = keep.tile([P, 2, 4], F32)
+        nc.sync.dma_start(out=s_col[:], in_=x_scale.rearrange("o (j p m) -> p (o j) m", j=2, m=4))
+        b_col = keep.tile([P, 4], BF16)
+        nc.sync.dma_start(out=b_col[:], in_=b1.rearrange("(p m) -> p m", m=4))
+
+        x_rows = x_bytes.rearrange("(p n) k -> p n k", n=NT)
+        prior_rows = prior.rearrange("(p n) k -> p n k", n=NT)
+        out_rows = out.rearrange("(p n) h -> p n h", n=NT)
+        x_fp8, prior_in = [None] * 4, [None] * 4
+
+        def load_x(q):
+            x_fp8[q] = keep.tile([P, 2, D], U8, name="x_fp8_%d" % q)
+            nc.sync.dma_start(out=x_fp8[q][:], in_=x_rows[:, 2 * q : 2 * q + 2, :])
+
+        def load_prior(q):
+            prior_in[q] = keep.tile([P, 2, PRIOR], BF16, name="prior_in_%d" % q)
+            nc.sync.dma_start(out=prior_in[q][:], in_=prior_rows[:, 2 * q : 2 * q + 2, :])
+
+        def load_scales(tile4, src):
+            for q in range(4):
+                nc.sync.dma_start(
+                    out=tile4[32 * q : 32 * q + 4, :, :].bitcast(I32),
+                    in_=src[:, 4 * q : 4 * q + 4, :].rearrange("g q n -> q g n").bitcast(I32),
+                )
+
+        load_x(0)
+        load_prior(0)
+        wp = keep.tile([P, 1, 2 * G], U8, align_bytes=64)
+        nc.sync.dma_start(out=wp[:].bitcast(I32), in_=wp_words.rearrange("g p b -> p g b").bitcast(I32))
+        wx = keep.tile([P, 2, 2 * G], U8, align_bytes=64)
+        nc.sync.dma_start(out=wx[:].bitcast(I32), in_=wx_words.rearrange("g p b -> p g b").bitcast(I32))
+        load_scales(a_scales[:, 0:1, :], wp_scales)
+        load_scales(a_scales[:, 1:3, :], wx_scales)
+        load_x(1)
+        load_prior(1)
+        wl = keep.tile([P, 2, 2 * HID], U8, align_bytes=64)
+        nc.sync.dma_start(out=wl[:].bitcast(I32), in_=wl_words.rearrange("g p b -> p g b").bitcast(I32))
+        w2 = keep.tile([P, 1, 2 * HID], U8, align_bytes=64)
+        nc.sync.dma_start(out=w2[:].bitcast(I32), in_=w2_words.rearrange("g p b -> p g b").bitcast(I32))
+        load_scales(wl_sc, wl_scales)
+        load_scales(w2_sc[:].rearrange("p (c n) -> p c n", c=1), w2_scales)
+        load_x(2)
+        load_prior(2)
+        load_x(3)
+        load_prior(3)
+
+        s_all = keep.tile([P, D], F32)
+        bias = keep.tile([P, 4, P], F32)
+
+        def bc():
+            for j in range(2):
+                spread = psum.tile([P, 4, P], F32, name="spread%d" % j, tag="tr", bufs=2)
+                for m in range(4):
+                    nc.tensor.transpose(spread[:, m, :], s_col[:, j, m : m + 1].to_broadcast([P, P]), ident[:])
+                nc.scalar.activation(
+                    out=s_all[:, 512 * j : 512 * (j + 1)].rearrange("c (p m) -> c p m", m=4),
+                    in_=spread[:].rearrange("c m p -> c p m"),
+                    func=ACT.Copy,
+                    scale=2.0,
+                )
+
+        def bb():
+            spread_b = psum.tile([P, 4, P], BF16, tag="r", bufs=1)
+            for m in range(4):
+                nc.tensor.transpose(spread_b[:, m, :], b_col[:, m : m + 1].to_broadcast([P, P]), ident_bf[:])
+            nc.scalar.copy(out=bias[:], in_=spread_b[:])
+
+        pd, tp, pg, pc, ps_ = {}, {}, {}, {}, {}
+
+        def double_prior(q):
+            pd[q] = work.tile([P, 2 * PRIOR], BF16, name="pd%d" % q, tag="pd", bufs=2)
+            nc.vector.tensor_scalar(
+                out=pd[q][:], in0=prior_in[q][:].rearrange("p n k -> p (n k)"), scalar1=2.0, scalar2=None, op0=ALU.mult
+            )
+
+        def turn_prior(q):
+            tp[q] = psum.tile([P, 2, 2, P], F32, name="tp%d" % q, tag="tr", bufs=2)
+            words = pd[q][:].bitcast(F32)
+            for i in range(2):
+                for u in range(2):
+                    nc.tensor.transpose(tp[q][:, i, u, :], words[:, 256 * i + u : 256 * (i + 1) : 2], ident[:])
+
+        def copy_prior(q):
+            pg[q] = work.tile([P, 2 * P * 4], BF16, name="pg%d" % q, tag="pg", bufs=2, align_bytes=64)
+            nc.scalar.copy(
+                out=pg[q][:].bitcast(F32).rearrange("p (i r u) -> p i r u", i=2, u=2),
+                in_=tp[q][:].rearrange("p i u r -> p i r u"),
+            )
+
+        def quant_prior(q):
+            pc[q] = keep.tile([P, 2 * P], U32, name="pc%d" % q, align_bytes=64)
+            ps_[q] = keep.tile([P, 2 * P], U8, name="ps%d" % q, align_bytes=64)
+            nc.vector.quantize_mx(out=pc[q][:].bitcast(FP8X4), scales=ps_[q][:], in_=pg[q][:])
+
+        xw, tx, xg, xc, xs = {}, {}, {}, {}, {}
+
+        def mul_x(n):
+            xw[n] = work.tile([P, D], BF16, name="xw%d" % n, tag="xw", bufs=3)
+            for c0, c1 in ((0, 512), (512, 1024)) if n == 0 else ((0, 1024),):
+                nc.vector.tensor_tensor(
+                    out=xw[n][:, c0:c1], in0=x_fp8[n // 2][:, n % 2, c0:c1].bitcast(FP8), in1=s_all[:, c0:c1], op=ALU.mult
+                )
+
+        def turn_x(n):
+            tx[n] = psum.tile([P, 2, 2, P], F32, name="tx%d" % n, tag="tr", bufs=2)
+            words = xw[n][:].bitcast(F32)
+            for g in range(2):
+                for u in range(2):
+                    nc.tensor.transpose(tx[n][:, g, u, :], words[:, 256 * g + u : 256 * (g + 1) : 2], ident[:])
+
+        def copy_x(n):
+            xg[n] = work.tile([P, 2 * P * 4], BF16, name="xg%d" % n, tag="xg", bufs=3, align_bytes=64)
+            nc.scalar.copy(
+                out=xg[n][:].bitcast(F32).rearrange("p (g r u) -> p g r u", g=2, u=2),
+                in_=tx[n][:].rearrange("p g u r -> p g r u"),
+            )
+
+        def quant_x(n):
+            xc[n] = keep.tile([P, 2 * P], U32, name="xc%d" % n, align_bytes=64)
+            xs[n] = keep.tile([P, 2 * P], U8, name="xs%d" % n, align_bytes=64)
+            nc.vector.quantize_mx(out=xc[n][:].bitcast(FP8X4), scales=xs[n][:], in_=xg[n][:])
+
+        acc_a, r_rows, tr_r, rg, rc, rs = {}, {}, {}, {}, {}, {}
+
+        def mm_a(n):
+            acc_a[n] = psum.tile([P, G], F32, name="acc_a%d" % n, tag="a", bufs=1)
+            c0 = P * (n % 2)
+            for i in range(3):
+                if i == 0:
+                    codes, scales, w = pc[n // 2][:, c0 : c0 + P], ps_[n // 2][:, c0 : c0 + P], wp[:, 0, :]
+                else:
+                    codes, scales, w = xc[n][:, P * (i - 1) : P * i], xs[n][:, P * (i - 1) : P * i], wx[:, i - 1, :]
+                nc.tensor.matmul_mx(
+                    out=acc_a[n][:], lhsT=codes.bitcast(FP8X4), lhsT_scale=scales, rhs=w.bitcast(FP4X4),
+                    rhs_scale=a_scales[:, i, :], start=(i == 0), stop=(i == 2),
+                )
+
+        def add_bias(n):
+            r_rows[n] = work.tile([P, 4, P], BF16, name="r_rows%d" % n, tag="r_rows", bufs=2)
+            nc.vector.scalar_tensor_tensor(
+                out=r_rows[n][:], in0=acc_a[n][:].rearrange("c (p t) -> c t p", t=4), scalar=0.5, in1=bias[:], op0=ALU.mult, op1=ALU.add
+            )
+
+        def turn_r(n):
+            tr_r[n] = psum.tile([P, 4, P], BF16, name="tr_r%d" % n, tag="r", bufs=1)
+            for t in range(4):
+                nc.tensor.transpose(tr_r[n][:, t, :], r_rows[n][:, t, :], ident_bf[:])
+
+        def relu_r(n):
+            rg[n] = work.tile([P, P * 4], BF16, name="rg%d" % n, tag="rg", bufs=2, align_bytes=64)
+            nc.scalar.activation(
+                out=rg[n][:].rearrange("p (c t) -> p c t", t=4), in_=tr_r[n][:].rearrange("p t c -> p c t"), func=ACT.Relu
+            )
+
+        def quant_r(n):
+            rc[n] = work.tile([P, P], U32, name="rc%d" % n, tag="rc", bufs=3, align_bytes=64)
+            rs[n] = work.tile([P, P], U8, name="rs%d" % n, tag="rs", bufs=3, align_bytes=64)
+            nc.vector.quantize_mx(out=rc[n][:].bitcast(FP8X4), scales=rs[n][:], in_=rg[n][:])
+
+        acc_t, acc_h, gate, res = {}, {}, {}, {}
+
+        def mm_t(n, j):
+            acc_t[n, j] = psum.tile([P, BANK], F32, name="acc_t%d_%d" % (n, j), tag="t", bufs=2)
+            nc.tensor.matmul_mx(
+                out=acc_t[n, j][:], lhsT=rc[n][:].bitcast(FP8X4), lhsT_scale=rs[n][:],
+                rhs=w2[:, 0, 1024 * j : 1024 * (j + 1)].bitcast(FP4X4), rhs_scale=w2_sc[:, BANK * j : BANK * (j + 1)], start=True, stop=True,
+            )
+
+        def sig(n, j):
+            gate[n, j] = work.tile([P, BANK], F32, name="gate%d_%d" % (n, j), tag="gate", bufs=6)
+            nc.scalar.activation(out=gate[n, j][:], in_=acc_t[n, j][:], func=ACT.Sigmoid)
+
+        def mm_h(n, j):
+            acc_h[n, j] = psum.tile([P, BANK], F32, name="acc_h%d_%d" % (n, j), tag="h", bufs=2)
+            for g in range(2):
+                nc.tensor.matmul_mx(
+                    out=acc_h[n, j][:], lhsT=xc[n][:, P * g : P * (g + 1)].bitcast(FP8X4), lhsT_scale=xs[n][:, P * g : P * (g + 1)],
+                    rhs=wl[:, g, 1024 * j : 1024 * (j + 1)].bitcast(FP4X4), rhs_scale=wl_sc[:, g, BANK * j : BANK * (j + 1)],
+                    start=(g == 0), stop=(g == 1),
+                )
+
+        def gate_h(n, j):
+            if j == 0:
+                res[n] = work.tile([P, HID], F32, name="res%d" % n, tag="res", bufs=3)
+            nc.vector.scalar_tensor_tensor(
+                out=res[n][:, BANK * j : BANK * (j + 1)], in0=acc_h[n, j][:], scalar=0.0, in1=gate[n, j][:], op0=ALU.max, op1=ALU.mult
+            )
+            if n == NT - 1:
+                nc.sync.dma_start(out=out_rows[:, n, BANK * j : BANK * (j + 1)], in_=res[n][:, BANK * j : BANK * (j + 1)])
+            elif j == 1:
+                nc.sync.dma_start(out=out_rows[:, n, :], in_=res[n][:])
+
+        def both(stage, n):
+            for j in range(2):
+                stage(n, j)
+
+        ctx.enter_context(tc.manual_schedule())
+        bc()
+        double_prior(0)
+        turn_prior(0)
+        bb()
+        copy_prior(0)
+        mul_x(0)
+        turn_x(0)
+        copy_x(0)
+        mul_x(1)
+        turn_x(1)
+        double_prior(1)
+        turn_prior(1)
+        copy_x(1)
+        copy_prior(1)
+        quant_x(0)
+        quant_prior(0)
+        mm_a(0)
+        mul_x(2)
+        quant_x(1)
+        add_bias(0)
+        mul_x(3)
+        for i in range(NT + 1):
+            if i + 2 < NT:
+                turn_x(i + 2)
+                copy_x(i + 2)
+            if i in (1, 3):
+                turn_prior((i + 3) // 2)
+            if i < NT:
+                turn_r(i)
+                relu_r(i)
+            if i in (1, 3):
+                copy_prior((i + 3) // 2)
+            if i > 0:
+                both(mm_t, i - 1)
+                both(sig, i - 1)
+            if i + 1 < NT:
+                mm_a(i + 1)
+            if i > 0:
+                both(mm_h, i - 1)
+            if i + 2 < NT:
+                quant_x(i + 2)
+            if i + 1 < NT:
+                add_bias(i + 1)
+            if i < NT:
+                quant_r(i)
+            if i in (0, 2, 4):
+                quant_prior((i + 2) // 2)
+            if i in (0, 2):
+                double_prior(i // 2 + 2)
+            if i + 4 < NT:
+                mul_x(i + 4)
+            if i > 0:
+                both(gate_h, i - 1)

@@ -59,10 +59,6 @@ def tile_pepnetpriorgatedhiddenlayer_w4_kernel(
             x_fp8[q] = keep.tile([P, 2, D], U8, name="x_fp8_%d" % q)
             nc.sync.dma_start(out=x_fp8[q][:], in_=x_rows[:, 2 * q : 2 * q + 2, :])
 
-        def load_prior(q):
-            prior_in[q] = keep.tile([P, 2, PRIOR], BF16, name="prior_in_%d" % q)
-            nc.sync.dma_start(out=prior_in[q][:], in_=prior_rows[:, 2 * q : 2 * q + 2, :])
-
         def load_scales(tile4, src):
             for q in range(4):
                 nc.sync.dma_start(
@@ -70,26 +66,30 @@ def tile_pepnetpriorgatedhiddenlayer_w4_kernel(
                     in_=src[:, 4 * q : 4 * q + 4, :].rearrange("g q n -> q g n").bitcast(I32),
                 )
 
+        def load_prior_on(q, engine):
+            prior_in[q] = keep.tile([P, 2, PRIOR], BF16, name="prior_in_%d" % q)
+            engine.dma_start(out=prior_in[q][:], in_=prior_rows[:, 2 * q : 2 * q + 2, :])
+
         load_x(0)
-        load_prior(0)
+        load_prior_on(0, nc.scalar)
+        load_x(1)
+        load_prior_on(1, nc.scalar)
         wp = keep.tile([P, 1, 2 * G], U8, align_bytes=64)
         nc.sync.dma_start(out=wp[:].bitcast(I32), in_=wp_words.rearrange("g p b -> p g b").bitcast(I32))
         wx = keep.tile([P, 2, 2 * G], U8, align_bytes=64)
         nc.sync.dma_start(out=wx[:].bitcast(I32), in_=wx_words.rearrange("g p b -> p g b").bitcast(I32))
         load_scales(a_scales[:, 0:1, :], wp_scales)
         load_scales(a_scales[:, 1:3, :], wx_scales)
-        load_x(1)
-        load_prior(1)
+        load_scales(wl_sc, wl_scales)
+        load_scales(w2_sc[:].rearrange("p (c n) -> p c n", c=1), w2_scales)
+        load_x(2)
         wl = keep.tile([P, 2, 2 * HID], U8, align_bytes=64)
         nc.sync.dma_start(out=wl[:].bitcast(I32), in_=wl_words.rearrange("g p b -> p g b").bitcast(I32))
         w2 = keep.tile([P, 1, 2 * HID], U8, align_bytes=64)
         nc.sync.dma_start(out=w2[:].bitcast(I32), in_=w2_words.rearrange("g p b -> p g b").bitcast(I32))
-        load_scales(wl_sc, wl_scales)
-        load_scales(w2_sc[:].rearrange("p (c n) -> p c n", c=1), w2_scales)
-        load_x(2)
-        load_prior(2)
+        load_prior_on(2, nc.sync)
         load_x(3)
-        load_prior(3)
+        load_prior_on(3, nc.sync)
 
         s_all = keep.tile([P, D], F32)
         bias = keep.tile([P, 4, P], F32)
@@ -274,12 +274,11 @@ def tile_pepnetpriorgatedhiddenlayer_w4_kernel(
                 relu_r(i)
             if i in (1, 3):
                 copy_prior((i + 3) // 2)
-            if i > 0:
-                both(mm_t, i - 1)
-                both(sig, i - 1)
             if i + 1 < NT:
                 mm_a(i + 1)
             if i > 0:
+                both(mm_t, i - 1)
+                both(sig, i - 1)
                 both(mm_h, i - 1)
             if i + 2 < NT:
                 quant_x(i + 2)

@@ -30,6 +30,8 @@ def tile_pepnetpriorgatedhiddenlayer_w4_kernel(
         work = ctx.enter_context(tc.tile_pool(name="work", bufs=3))
         psum = ctx.enter_context(tc.psum_pool(name="psum", bufs=1))
 
+        warm = keep.tile([P, BANK], BF16)
+        nc.vector.memset(warm[:], 0.0)
         dummy = keep.tile([P, 1], F32)
         nc.vector.memset(dummy[:], 0.0)
         nc.scalar.activation(out=dummy[:], in_=dummy[:], func=ACT.Sigmoid)
@@ -47,8 +49,6 @@ def tile_pepnetpriorgatedhiddenlayer_w4_kernel(
 
         s_col = keep.tile([P, 2, 4], F32)
         nc.sync.dma_start(out=s_col[:], in_=x_scale.rearrange("o (j p m) -> p (o j) m", j=2, m=4))
-        b_col = keep.tile([P, 4], BF16)
-        nc.sync.dma_start(out=b_col[:], in_=b1.rearrange("(p m) -> p m", m=4))
 
         x_rows = x_bytes.rearrange("(p n) k -> p n k", n=NT)
         prior_rows = prior.rearrange("(p n) k -> p n k", n=NT)
@@ -73,26 +73,28 @@ def tile_pepnetpriorgatedhiddenlayer_w4_kernel(
         load_x(0)
         load_prior_on(0, nc.scalar)
         load_x(1)
-        load_prior_on(1, nc.scalar)
-        wp = keep.tile([P, 1, 2 * G], U8, align_bytes=64)
-        nc.sync.dma_start(out=wp[:].bitcast(I32), in_=wp_words.rearrange("g p b -> p g b").bitcast(I32))
+        load_scales(a_scales[:, 1:3, :], wx_scales)
         wx = keep.tile([P, 2, 2 * G], U8, align_bytes=64)
         nc.sync.dma_start(out=wx[:].bitcast(I32), in_=wx_words.rearrange("g p b -> p g b").bitcast(I32))
+        wp = keep.tile([P, 1, 2 * G], U8, align_bytes=64)
+        nc.sync.dma_start(out=wp[:].bitcast(I32), in_=wp_words.rearrange("g p b -> p g b").bitcast(I32))
         load_scales(a_scales[:, 0:1, :], wp_scales)
-        load_scales(a_scales[:, 1:3, :], wx_scales)
-        load_scales(wl_sc, wl_scales)
+        b_col = keep.tile([P, 4], BF16)
+        nc.sync.dma_start(out=b_col[:], in_=b1.rearrange("(p m) -> p m", m=4))
+        load_prior_on(1, nc.sync)
         load_scales(w2_sc[:].rearrange("p (c n) -> p c n", c=1), w2_scales)
+        load_scales(wl_sc, wl_scales)
+        w2 = keep.tile([P, 1, 2 * HID], U8, align_bytes=64)
+        nc.sync.dma_start(out=w2[:].bitcast(I32), in_=w2_words.rearrange("g p b -> p g b").bitcast(I32))
         load_x(2)
         wl = keep.tile([P, 2, 2 * HID], U8, align_bytes=64)
         nc.sync.dma_start(out=wl[:].bitcast(I32), in_=wl_words.rearrange("g p b -> p g b").bitcast(I32))
-        w2 = keep.tile([P, 1, 2 * HID], U8, align_bytes=64)
-        nc.sync.dma_start(out=w2[:].bitcast(I32), in_=w2_words.rearrange("g p b -> p g b").bitcast(I32))
         load_prior_on(2, nc.sync)
         load_x(3)
         load_prior_on(3, nc.sync)
 
         s_all = keep.tile([P, D], F32)
-        bias = keep.tile([P, 4, P], F32)
+        bias = keep.tile([P, 2, P, 2], F32)
 
         def bc():
             for j in range(2):
@@ -110,7 +112,9 @@ def tile_pepnetpriorgatedhiddenlayer_w4_kernel(
             spread_b = psum.tile([P, 4, P], BF16, tag="r", bufs=1)
             for m in range(4):
                 nc.tensor.transpose(spread_b[:, m, :], b_col[:, m : m + 1].to_broadcast([P, P]), ident_bf[:])
-            nc.scalar.copy(out=bias[:], in_=spread_b[:])
+            nc.scalar.activation(
+                out=bias[:], in_=spread_b[:].rearrange("c (u e) p -> c u p e", u=2), func=ACT.Copy, scale=2.0
+            )
 
         pd, tp, pg, pc, ps_ = {}, {}, {}, {}, {}
 
@@ -122,17 +126,27 @@ def tile_pepnetpriorgatedhiddenlayer_w4_kernel(
 
         def turn_prior(q):
             tp[q] = psum.tile([P, 2, 2, P], F32, name="tp%d" % q, tag="tr", bufs=2)
-            words = pd[q][:].bitcast(F32)
+            src = pd[q][:] if q < 2 else prior_in[q][:].rearrange("p n k -> p (n k)")
+            words = src.bitcast(F32)
             for i in range(2):
                 for u in range(2):
                     nc.tensor.transpose(tp[q][:, i, u, :], words[:, 256 * i + u : 256 * (i + 1) : 2], ident[:])
 
         def copy_prior(q):
             pg[q] = work.tile([P, 2 * P * 4], BF16, name="pg%d" % q, tag="pg", bufs=2, align_bytes=64)
-            nc.scalar.copy(
-                out=pg[q][:].bitcast(F32).rearrange("p (i r u) -> p i r u", i=2, u=2),
-                in_=tp[q][:].rearrange("p i u r -> p i r u"),
-            )
+            if q < 2:
+                nc.scalar.copy(
+                    out=pg[q][:].bitcast(F32).rearrange("p (i r u) -> p i r u", i=2, u=2),
+                    in_=tp[q][:].rearrange("p i u r -> p i r u"),
+                )
+            else:
+                for i in range(2):
+                    nc.scalar.activation(
+                        out=pg[q][:, 512 * i : 512 * (i + 1)].rearrange("p (r u e) -> p r u e", u=2, e=2),
+                        in_=tp[q][:, i, :, :].rearrange("p u r -> p (u r)").bitcast(BF16).rearrange("p (u r e) -> p r u e", u=2, e=2),
+                        func=ACT.Copy,
+                        scale=2.0,
+                    )
 
         def quant_prior(q):
             pc[q] = keep.tile([P, 2 * P], U32, name="pc%d" % q, align_bytes=64)
@@ -183,20 +197,23 @@ def tile_pepnetpriorgatedhiddenlayer_w4_kernel(
                 )
 
         def add_bias(n):
-            r_rows[n] = work.tile([P, 4, P], BF16, name="r_rows%d" % n, tag="r_rows", bufs=2)
-            nc.vector.scalar_tensor_tensor(
-                out=r_rows[n][:], in0=acc_a[n][:].rearrange("c (p t) -> c t p", t=4), scalar=0.5, in1=bias[:], op0=ALU.mult, op1=ALU.add
+            r_rows[n] = work.tile([P, 2, P, 2], BF16, name="r_rows%d" % n, tag="r_rows", bufs=2)
+            nc.vector.tensor_tensor(
+                out=r_rows[n][:], in0=acc_a[n][:].rearrange("c (p u e) -> c u p e", u=2, e=2), in1=bias[:], op=ALU.add
             )
 
         def turn_r(n):
-            tr_r[n] = psum.tile([P, 4, P], BF16, name="tr_r%d" % n, tag="r", bufs=1)
-            for t in range(4):
-                nc.tensor.transpose(tr_r[n][:, t, :], r_rows[n][:, t, :], ident_bf[:])
+            tr_r[n] = psum.tile([P, 2 * P], F32, name="tr_r%d" % n, tag="r", bufs=1)
+            words = r_rows[n][:].rearrange("c u p e -> c (u p e)").bitcast(F32)
+            for u in range(2):
+                nc.tensor.transpose(tr_r[n][:, P * u : P * (u + 1)], words[:, P * u : P * (u + 1)], ident[:])
 
         def relu_r(n):
             rg[n] = work.tile([P, P * 4], BF16, name="rg%d" % n, tag="rg", bufs=2, align_bytes=64)
             nc.scalar.activation(
-                out=rg[n][:].rearrange("p (c t) -> p c t", t=4), in_=tr_r[n][:].rearrange("p t c -> p c t"), func=ACT.Relu
+                out=rg[n][:].rearrange("p (c u e) -> p c u e", u=2, e=2),
+                in_=tr_r[n][:].bitcast(BF16).rearrange("p (u c e) -> p c u e", u=2, e=2),
+                func=ACT.Relu,
             )
 
         def quant_r(n):
@@ -215,7 +232,7 @@ def tile_pepnetpriorgatedhiddenlayer_w4_kernel(
 
         def sig(n, j):
             gate[n, j] = work.tile([P, BANK], F32, name="gate%d_%d" % (n, j), tag="gate", bufs=6)
-            nc.scalar.activation(out=gate[n, j][:], in_=acc_t[n, j][:], func=ACT.Sigmoid)
+            nc.scalar.activation(out=gate[n, j][:], in_=acc_t[n, j][:], func=ACT.Sigmoid, scale=0.5)
 
         def mm_h(n, j):
             acc_h[n, j] = psum.tile([P, BANK], F32, name="acc_h%d_%d" % (n, j), tag="h", bufs=2)
@@ -237,23 +254,32 @@ def tile_pepnetpriorgatedhiddenlayer_w4_kernel(
             elif j == 1:
                 nc.sync.dma_start(out=out_rows[:, n, :], in_=res[n][:])
 
+        def warm_up(count):
+            for i in range(count):
+                junk = psum.tile([P, BANK], F32, name="junk", tag="t", bufs=2)
+                nc.tensor.matmul(junk[:], warm[:, 0:P], warm[:], start=True, stop=True)
+
         def both(stage, n):
             for j in range(2):
                 stage(n, j)
 
         ctx.enter_context(tc.manual_schedule())
+        warm_up(5)
         bc()
         double_prior(0)
         turn_prior(0)
-        bb()
+        warm_up(2)
         copy_prior(0)
         mul_x(0)
         turn_x(0)
         copy_x(0)
+        warm_up(2)
         mul_x(1)
         turn_x(1)
         double_prior(1)
         turn_prior(1)
+        warm_up(1)
+        bb()
         copy_x(1)
         copy_prior(1)
         quant_x(0)
@@ -288,8 +314,6 @@ def tile_pepnetpriorgatedhiddenlayer_w4_kernel(
                 quant_r(i)
             if i in (0, 2, 4):
                 quant_prior((i + 2) // 2)
-            if i in (0, 2):
-                double_prior(i // 2 + 2)
             if i + 4 < NT:
                 mul_x(i + 4)
             if i > 0:

@@ -6,6 +6,7 @@ from concourse.masks import make_identity
 P = 128
 TOKENS, D, PRIOR, G, HID = 1024, 1024, 512, 512, 1024
 NT = TOKENS // P
+PAIRS = NT // 2
 BANK = 512
 FLOPS = 2 * TOKENS * (D * G + PRIOR * G + G * HID + D * HID)
 
@@ -53,26 +54,27 @@ def tile_pepnetpriorgatedhiddenlayer_w4_kernel(
         x_rows = x_bytes.rearrange("(p n) k -> p n k", n=NT)
         prior_rows = prior.rearrange("(p n) k -> p n k", n=NT)
         out_rows = out.rearrange("(p n) h -> p n h", n=NT)
-        x_fp8, prior_in = [None] * 4, [None] * 4
+        x_fp8, prior_in = [None] * PAIRS, [None] * PAIRS
 
         def load_x(q):
             x_fp8[q] = keep.tile([P, 2, D], U8, name="x_fp8_%d" % q)
             nc.sync.dma_start(out=x_fp8[q][:], in_=x_rows[:, 2 * q : 2 * q + 2, :])
 
-        def load_scales(tile4, src):
-            for q in range(4):
-                nc.sync.dma_start(
-                    out=tile4[32 * q : 32 * q + 4, :, :].bitcast(I32),
-                    in_=src[:, 4 * q : 4 * q + 4, :].rearrange("g q n -> q g n").bitcast(I32),
-                )
-
-        def load_prior_on(q, engine):
+        def load_prior(q, engine):
             prior_in[q] = keep.tile([P, 2, PRIOR], BF16, name="prior_in_%d" % q)
             engine.dma_start(out=prior_in[q][:], in_=prior_rows[:, 2 * q : 2 * q + 2, :])
 
+        def load_scales(scale_tile, src):
+            for quad in range(4):
+                nc.sync.dma_start(
+                    out=scale_tile[32 * quad : 32 * quad + 4, :, :].bitcast(I32),
+                    in_=src[:, 4 * quad : 4 * quad + 4, :].rearrange("g q n -> q g n").bitcast(I32),
+                )
+
         load_x(0)
-        load_prior_on(0, nc.scalar)
+        load_prior(0, nc.scalar)
         load_x(1)
+        load_prior(1, nc.scalar)
         load_scales(a_scales[:, 1:3, :], wx_scales)
         wx = keep.tile([P, 2, 2 * G], U8, align_bytes=64)
         nc.sync.dma_start(out=wx[:].bitcast(I32), in_=wx_words.rearrange("g p b -> p g b").bitcast(I32))
@@ -81,7 +83,6 @@ def tile_pepnetpriorgatedhiddenlayer_w4_kernel(
         load_scales(a_scales[:, 0:1, :], wp_scales)
         b_col = keep.tile([P, 4], BF16)
         nc.sync.dma_start(out=b_col[:], in_=b1.rearrange("(p m) -> p m", m=4))
-        load_prior_on(1, nc.sync)
         load_scales(w2_sc[:].rearrange("p (c n) -> p c n", c=1), w2_scales)
         load_scales(wl_sc, wl_scales)
         w2 = keep.tile([P, 1, 2 * HID], U8, align_bytes=64)
@@ -89,26 +90,27 @@ def tile_pepnetpriorgatedhiddenlayer_w4_kernel(
         load_x(2)
         wl = keep.tile([P, 2, 2 * HID], U8, align_bytes=64)
         nc.sync.dma_start(out=wl[:].bitcast(I32), in_=wl_words.rearrange("g p b -> p g b").bitcast(I32))
-        load_prior_on(2, nc.sync)
+        load_prior(2, nc.sync)
         load_x(3)
-        load_prior_on(3, nc.sync)
+        load_prior(3, nc.sync)
 
         s_all = keep.tile([P, D], F32)
         bias = keep.tile([P, 2, P, 2], F32)
 
-        def bc():
+        def spread_scales():
             for j in range(2):
                 spread = psum.tile([P, 4, P], F32, name="spread%d" % j, tag="tr", bufs=2)
                 for m in range(4):
                     nc.tensor.transpose(spread[:, m, :], s_col[:, j, m : m + 1].to_broadcast([P, P]), ident[:])
-                nc.scalar.activation(
-                    out=s_all[:, 512 * j : 512 * (j + 1)].rearrange("c (p m) -> c p m", m=4),
-                    in_=spread[:].rearrange("c m p -> c p m"),
-                    func=ACT.Copy,
-                    scale=2.0,
-                )
+                for p0, p1 in ((0, P // 2), (P // 2, P)) if j == 0 else ((0, P),):
+                    nc.scalar.activation(
+                        out=s_all[:, 512 * j + 4 * p0 : 512 * j + 4 * p1].rearrange("c (p m) -> c p m", m=4),
+                        in_=spread[:, :, p0:p1].rearrange("c m p -> c p m"),
+                        func=ACT.Copy,
+                        scale=2.0,
+                    )
 
-        def bb():
+        def spread_bias():
             spread_b = psum.tile([P, 4, P], BF16, tag="r", bufs=1)
             for m in range(4):
                 nc.tensor.transpose(spread_b[:, m, :], b_col[:, m : m + 1].to_broadcast([P, P]), ident_bf[:])
@@ -116,81 +118,68 @@ def tile_pepnetpriorgatedhiddenlayer_w4_kernel(
                 out=bias[:], in_=spread_b[:].rearrange("c (u e) p -> c u p e", u=2), func=ACT.Copy, scale=2.0
             )
 
-        pd, tp, pg, pc, ps_ = {}, {}, {}, {}, {}
+        prior_t, prior_grouped, prior_codes, prior_mx_scales = {}, {}, {}, {}
 
-        def double_prior(q):
-            pd[q] = work.tile([P, 2 * PRIOR], BF16, name="pd%d" % q, tag="pd", bufs=2)
-            nc.vector.tensor_scalar(
-                out=pd[q][:], in0=prior_in[q][:].rearrange("p n k -> p (n k)"), scalar1=2.0, scalar2=None, op0=ALU.mult
-            )
-
-        def turn_prior(q):
-            tp[q] = psum.tile([P, 2, 2, P], F32, name="tp%d" % q, tag="tr", bufs=2)
-            src = pd[q][:] if q < 2 else prior_in[q][:].rearrange("p n k -> p (n k)")
-            words = src.bitcast(F32)
+        def transpose_prior(q):
+            prior_t[q] = psum.tile([P, 2, 2, P], F32, name="prior_t%d" % q, tag="h" if q == 1 else "tr", bufs=2)
+            words = prior_in[q][:].rearrange("p n k -> p (n k)").bitcast(F32)
             for i in range(2):
                 for u in range(2):
-                    nc.tensor.transpose(tp[q][:, i, u, :], words[:, 256 * i + u : 256 * (i + 1) : 2], ident[:])
+                    nc.tensor.transpose(prior_t[q][:, i, u, :], words[:, 256 * i + u : 256 * (i + 1) : 2], ident[:])
 
         def copy_prior(q):
-            pg[q] = work.tile([P, 2 * P * 4], BF16, name="pg%d" % q, tag="pg", bufs=2, align_bytes=64)
-            if q < 2:
-                nc.scalar.copy(
-                    out=pg[q][:].bitcast(F32).rearrange("p (i r u) -> p i r u", i=2, u=2),
-                    in_=tp[q][:].rearrange("p i u r -> p i r u"),
+            prior_grouped[q] = work.tile([P, 2 * P * 4], BF16, name="prior_grouped%d" % q, tag="prior_grouped", bufs=2, align_bytes=64)
+            for i in range(2):
+                nc.scalar.activation(
+                    out=prior_grouped[q][:, 512 * i : 512 * (i + 1)].rearrange("p (r u e) -> p r u e", u=2, e=2),
+                    in_=prior_t[q][:, i, :, :].rearrange("p u r -> p (u r)").bitcast(BF16).rearrange("p (u r e) -> p r u e", u=2, e=2),
+                    func=ACT.Copy,
+                    scale=2.0,
                 )
-            else:
-                for i in range(2):
-                    nc.scalar.activation(
-                        out=pg[q][:, 512 * i : 512 * (i + 1)].rearrange("p (r u e) -> p r u e", u=2, e=2),
-                        in_=tp[q][:, i, :, :].rearrange("p u r -> p (u r)").bitcast(BF16).rearrange("p (u r e) -> p r u e", u=2, e=2),
-                        func=ACT.Copy,
-                        scale=2.0,
-                    )
 
-        def quant_prior(q):
-            pc[q] = keep.tile([P, 2 * P], U32, name="pc%d" % q, align_bytes=64)
-            ps_[q] = keep.tile([P, 2 * P], U8, name="ps%d" % q, align_bytes=64)
-            nc.vector.quantize_mx(out=pc[q][:].bitcast(FP8X4), scales=ps_[q][:], in_=pg[q][:])
+        def quantize_prior(q):
+            prior_codes[q] = keep.tile([P, 2 * P], U32, name="prior_codes%d" % q, align_bytes=64)
+            prior_mx_scales[q] = keep.tile([P, 2 * P], U8, name="prior_mx_scales%d" % q, align_bytes=64)
+            nc.vector.quantize_mx(out=prior_codes[q][:].bitcast(FP8X4), scales=prior_mx_scales[q][:], in_=prior_grouped[q][:])
 
-        xw, tx, xg, xc, xs = {}, {}, {}, {}, {}
+        x_scaled, x_t, x_grouped, x_codes, x_mx_scales = {}, {}, {}, {}, {}
 
-        def mul_x(n):
-            xw[n] = work.tile([P, D], BF16, name="xw%d" % n, tag="xw", bufs=3)
-            for c0, c1 in ((0, 512), (512, 1024)) if n == 0 else ((0, 1024),):
+        def scale_x(n):
+            x_scaled[n] = work.tile([P, D], BF16, name="x_scaled%d" % n, tag="x_scaled", bufs=3)
+            for c0, c1 in ((0, 256), (256, 512), (512, 1024)) if n == 0 else ((0, 1024),):
                 nc.vector.tensor_tensor(
-                    out=xw[n][:, c0:c1], in0=x_fp8[n // 2][:, n % 2, c0:c1].bitcast(FP8), in1=s_all[:, c0:c1], op=ALU.mult
+                    out=x_scaled[n][:, c0:c1], in0=x_fp8[n // 2][:, n % 2, c0:c1].bitcast(FP8), in1=s_all[:, c0:c1], op=ALU.mult
                 )
 
-        def turn_x(n):
-            tx[n] = psum.tile([P, 2, 2, P], F32, name="tx%d" % n, tag="tr", bufs=2)
-            words = xw[n][:].bitcast(F32)
+        def transpose_x(n):
+            x_t[n] = psum.tile([P, 2, 2, P], F32, name="x_t%d" % n, tag="tr", bufs=2)
+            words = x_scaled[n][:].bitcast(F32)
             for g in range(2):
                 for u in range(2):
-                    nc.tensor.transpose(tx[n][:, g, u, :], words[:, 256 * g + u : 256 * (g + 1) : 2], ident[:])
+                    nc.tensor.transpose(x_t[n][:, g, u, :], words[:, 256 * g + u : 256 * (g + 1) : 2], ident[:])
 
         def copy_x(n):
-            xg[n] = work.tile([P, 2 * P * 4], BF16, name="xg%d" % n, tag="xg", bufs=3, align_bytes=64)
+            x_grouped[n] = work.tile([P, 2 * P * 4], BF16, name="x_grouped%d" % n, tag="x_grouped", bufs=3, align_bytes=64)
             nc.scalar.copy(
-                out=xg[n][:].bitcast(F32).rearrange("p (g r u) -> p g r u", g=2, u=2),
-                in_=tx[n][:].rearrange("p g u r -> p g r u"),
+                out=x_grouped[n][:].bitcast(F32).rearrange("p (g r u) -> p g r u", g=2, u=2),
+                in_=x_t[n][:].rearrange("p g u r -> p g r u"),
             )
 
-        def quant_x(n):
-            xc[n] = keep.tile([P, 2 * P], U32, name="xc%d" % n, align_bytes=64)
-            xs[n] = keep.tile([P, 2 * P], U8, name="xs%d" % n, align_bytes=64)
-            nc.vector.quantize_mx(out=xc[n][:].bitcast(FP8X4), scales=xs[n][:], in_=xg[n][:])
+        def quantize_x(n):
+            x_codes[n] = keep.tile([P, 2 * P], U32, name="x_codes%d" % n, align_bytes=64)
+            x_mx_scales[n] = keep.tile([P, 2 * P], U8, name="x_mx_scales%d" % n, align_bytes=64)
+            nc.vector.quantize_mx(out=x_codes[n][:].bitcast(FP8X4), scales=x_mx_scales[n][:], in_=x_grouped[n][:])
 
-        acc_a, r_rows, tr_r, rg, rc, rs = {}, {}, {}, {}, {}, {}
+        acc_a, r_rows, r_t, r_grouped, r_codes, r_mx_scales = {}, {}, {}, {}, {}, {}
 
-        def mm_a(n):
+        def matmul_a(n):
             acc_a[n] = psum.tile([P, G], F32, name="acc_a%d" % n, tag="a", bufs=1)
             c0 = P * (n % 2)
             for i in range(3):
                 if i == 0:
-                    codes, scales, w = pc[n // 2][:, c0 : c0 + P], ps_[n // 2][:, c0 : c0 + P], wp[:, 0, :]
+                    codes, scales, w = prior_codes[n // 2][:, c0 : c0 + P], prior_mx_scales[n // 2][:, c0 : c0 + P], wp[:, 0, :]
                 else:
-                    codes, scales, w = xc[n][:, P * (i - 1) : P * i], xs[n][:, P * (i - 1) : P * i], wx[:, i - 1, :]
+                    codes, scales, w = x_codes[n][:, P * (i - 1) : P * i], x_mx_scales[n][:, P * (i - 1) : P * i], wx[:, i - 1, :]
                 nc.tensor.matmul_mx(
                     out=acc_a[n][:], lhsT=codes.bitcast(FP8X4), lhsT_scale=scales, rhs=w.bitcast(FP4X4),
                     rhs_scale=a_scales[:, i, :], start=(i == 0), stop=(i == 2),
@@ -202,48 +191,49 @@ def tile_pepnetpriorgatedhiddenlayer_w4_kernel(
                 out=r_rows[n][:], in0=acc_a[n][:].rearrange("c (p u e) -> c u p e", u=2, e=2), in1=bias[:], op=ALU.add
             )
 
-        def turn_r(n):
-            tr_r[n] = psum.tile([P, 2 * P], F32, name="tr_r%d" % n, tag="r", bufs=1)
+        def transpose_r(n):
+            r_t[n] = psum.tile([P, 2 * P], F32, name="r_t%d" % n, tag="r", bufs=1)
             words = r_rows[n][:].rearrange("c u p e -> c (u p e)").bitcast(F32)
             for u in range(2):
-                nc.tensor.transpose(tr_r[n][:, P * u : P * (u + 1)], words[:, P * u : P * (u + 1)], ident[:])
+                nc.tensor.transpose(r_t[n][:, P * u : P * (u + 1)], words[:, P * u : P * (u + 1)], ident[:])
 
         def relu_r(n):
-            rg[n] = work.tile([P, P * 4], BF16, name="rg%d" % n, tag="rg", bufs=2, align_bytes=64)
+            r_grouped[n] = work.tile([P, P * 4], BF16, name="r_grouped%d" % n, tag="r_grouped", bufs=2, align_bytes=64)
             nc.scalar.activation(
-                out=rg[n][:].rearrange("p (c u e) -> p c u e", u=2, e=2),
-                in_=tr_r[n][:].bitcast(BF16).rearrange("p (u c e) -> p c u e", u=2, e=2),
+                out=r_grouped[n][:].rearrange("p (c u e) -> p c u e", u=2, e=2),
+                in_=r_t[n][:].bitcast(BF16).rearrange("p (u c e) -> p c u e", u=2, e=2),
                 func=ACT.Relu,
             )
 
-        def quant_r(n):
-            rc[n] = work.tile([P, P], U32, name="rc%d" % n, tag="rc", bufs=3, align_bytes=64)
-            rs[n] = work.tile([P, P], U8, name="rs%d" % n, tag="rs", bufs=3, align_bytes=64)
-            nc.vector.quantize_mx(out=rc[n][:].bitcast(FP8X4), scales=rs[n][:], in_=rg[n][:])
+        def quantize_r(n):
+            r_codes[n] = work.tile([P, P], U32, name="r_codes%d" % n, tag="r_codes", bufs=3, align_bytes=64)
+            r_mx_scales[n] = work.tile([P, P], U8, name="r_mx_scales%d" % n, tag="r_mx_scales", bufs=3, align_bytes=64)
+            nc.vector.quantize_mx(out=r_codes[n][:].bitcast(FP8X4), scales=r_mx_scales[n][:], in_=r_grouped[n][:])
 
         acc_t, acc_h, gate, res = {}, {}, {}, {}
 
-        def mm_t(n, j):
+        def matmul_t(n, j):
             acc_t[n, j] = psum.tile([P, BANK], F32, name="acc_t%d_%d" % (n, j), tag="t", bufs=2)
             nc.tensor.matmul_mx(
-                out=acc_t[n, j][:], lhsT=rc[n][:].bitcast(FP8X4), lhsT_scale=rs[n][:],
-                rhs=w2[:, 0, 1024 * j : 1024 * (j + 1)].bitcast(FP4X4), rhs_scale=w2_sc[:, BANK * j : BANK * (j + 1)], start=True, stop=True,
+                out=acc_t[n, j][:], lhsT=r_codes[n][:].bitcast(FP8X4), lhsT_scale=r_mx_scales[n][:],
+                rhs=w2[:, 0, 2 * BANK * j : 2 * BANK * (j + 1)].bitcast(FP4X4), rhs_scale=w2_sc[:, BANK * j : BANK * (j + 1)],
+                start=True, stop=True,
             )
 
-        def sig(n, j):
+        def sigmoid_t(n, j):
             gate[n, j] = work.tile([P, BANK], F32, name="gate%d_%d" % (n, j), tag="gate", bufs=6)
             nc.scalar.activation(out=gate[n, j][:], in_=acc_t[n, j][:], func=ACT.Sigmoid, scale=0.5)
 
-        def mm_h(n, j):
+        def matmul_h(n, j):
             acc_h[n, j] = psum.tile([P, BANK], F32, name="acc_h%d_%d" % (n, j), tag="h", bufs=2)
             for g in range(2):
                 nc.tensor.matmul_mx(
-                    out=acc_h[n, j][:], lhsT=xc[n][:, P * g : P * (g + 1)].bitcast(FP8X4), lhsT_scale=xs[n][:, P * g : P * (g + 1)],
-                    rhs=wl[:, g, 1024 * j : 1024 * (j + 1)].bitcast(FP4X4), rhs_scale=wl_sc[:, g, BANK * j : BANK * (j + 1)],
+                    out=acc_h[n, j][:], lhsT=x_codes[n][:, P * g : P * (g + 1)].bitcast(FP8X4), lhsT_scale=x_mx_scales[n][:, P * g : P * (g + 1)],
+                    rhs=wl[:, g, 2 * BANK * j : 2 * BANK * (j + 1)].bitcast(FP4X4), rhs_scale=wl_sc[:, g, BANK * j : BANK * (j + 1)],
                     start=(g == 0), stop=(g == 1),
                 )
 
-        def gate_h(n, j):
+        def gate_and_store(n, j):
             if j == 0:
                 res[n] = work.tile([P, HID], F32, name="res%d" % n, tag="res", bufs=3)
             nc.vector.scalar_tensor_tensor(
@@ -254,67 +244,63 @@ def tile_pepnetpriorgatedhiddenlayer_w4_kernel(
             elif j == 1:
                 nc.sync.dma_start(out=out_rows[:, n, :], in_=res[n][:])
 
-        def warm_up(count):
+        def keep_tensor_busy(count):
             for i in range(count):
                 junk = psum.tile([P, BANK], F32, name="junk", tag="t", bufs=2)
                 nc.tensor.matmul(junk[:], warm[:, 0:P], warm[:], start=True, stop=True)
 
-        def both(stage, n):
+        def both_halves(stage, n):
             for j in range(2):
                 stage(n, j)
 
         ctx.enter_context(tc.manual_schedule())
-        warm_up(5)
-        bc()
-        double_prior(0)
-        turn_prior(0)
-        warm_up(2)
+        keep_tensor_busy(3)
+        spread_scales()
+        transpose_prior(0)
         copy_prior(0)
-        mul_x(0)
-        turn_x(0)
+        keep_tensor_busy(3)
+        scale_x(0)
+        transpose_x(0)
         copy_x(0)
-        warm_up(2)
-        mul_x(1)
-        turn_x(1)
-        double_prior(1)
-        turn_prior(1)
-        warm_up(1)
-        bb()
+        scale_x(1)
+        quantize_prior(0)
+        transpose_prior(1)
+        transpose_x(1)
         copy_x(1)
+        quantize_x(0)
+        spread_bias()
         copy_prior(1)
-        quant_x(0)
-        quant_prior(0)
-        mm_a(0)
-        mul_x(2)
-        quant_x(1)
+        matmul_a(0)
+        scale_x(2)
         add_bias(0)
-        mul_x(3)
+        quantize_x(1)
+        scale_x(3)
         for i in range(NT + 1):
             if i + 2 < NT:
-                turn_x(i + 2)
+                transpose_x(i + 2)
                 copy_x(i + 2)
-            if i in (1, 3):
-                turn_prior((i + 3) // 2)
             if i < NT:
-                turn_r(i)
+                transpose_r(i)
                 relu_r(i)
-            if i in (1, 3):
+            if i % 2 == 1 and (i + 3) // 2 < PAIRS:
+                transpose_prior((i + 3) // 2)
                 copy_prior((i + 3) // 2)
-            if i + 1 < NT:
-                mm_a(i + 1)
             if i > 0:
-                both(mm_t, i - 1)
-                both(sig, i - 1)
-                both(mm_h, i - 1)
-            if i + 2 < NT:
-                quant_x(i + 2)
+                both_halves(matmul_t, i - 1)
+                both_halves(sigmoid_t, i - 1)
+            if i + 1 < NT:
+                matmul_a(i + 1)
+            if i > 0:
+                both_halves(matmul_h, i - 1)
             if i + 1 < NT:
                 add_bias(i + 1)
             if i < NT:
-                quant_r(i)
-            if i in (0, 2, 4):
-                quant_prior((i + 2) // 2)
-            if i + 4 < NT:
-                mul_x(i + 4)
+                quantize_r(i)
+            if i % 2 == 0 and (i + 2) // 2 < PAIRS:
+                quantize_prior((i + 2) // 2)
+            if i + 2 < NT:
+                quantize_x(i + 2)
             if i > 0:
-                both(gate_h, i - 1)
+                both_halves(gate_and_store, i - 1)
+            if i + 4 < NT:
+                scale_x(i + 4)

from contextlib import ExitStack

import concourse.mybir as mybir
from concourse.masks import make_identity

P = 128
TOKENS, D, PRIOR, G, HID = 1024, 1024, 512, 512, 1024
NT = TOKENS // P
PAIRS = NT // 2
BANK = 512
FLOPS = 2 * TOKENS * (D * G + PRIOR * G + G * HID + D * HID)

F32 = mybir.dt.float32
BF16 = mybir.dt.bfloat16
I32 = mybir.dt.int32
U32 = mybir.dt.uint32
U8 = mybir.dt.uint8
FP8 = mybir.dt.float8_e4m3fn
FP8X4 = mybir.dt.float8_e4m3fn_x4
FP4X4 = mybir.dt.float4_e2m1fn_x4
ACT = mybir.ActivationFunctionType
ALU = mybir.AluOpType


def tile_pepnetpriorgatedhiddenlayer_w4_kernel(
    tc, x_bytes, x_scale, prior, wx_words, wx_scales, wp_words, wp_scales, b1, w2_words, w2_scales, wl_words, wl_scales, out
):
    nc = tc.nc
    with ExitStack() as ctx:
        keep = ctx.enter_context(tc.tile_pool(name="keep", bufs=1))
        work = ctx.enter_context(tc.tile_pool(name="work", bufs=3))
        psum = ctx.enter_context(tc.psum_pool(name="psum", bufs=1))

        warm = keep.tile([P, BANK], BF16)
        nc.vector.memset(warm[:], 0.0)
        dummy = keep.tile([P, 1], F32)
        nc.vector.memset(dummy[:], 0.0)
        nc.scalar.activation(out=dummy[:], in_=dummy[:], func=ACT.Sigmoid)
        ident = keep.tile([P, P], F32)
        make_identity(nc, ident[:])
        ident_bf = keep.tile([P, P], BF16)
        nc.gpsimd.tensor_copy(out=ident_bf[:], in_=ident[:])

        a_scales = keep.tile([P, 3, G], U8, align_bytes=64)
        w2_sc = keep.tile([P, HID], U8, align_bytes=64)
        wl_sc = keep.tile([P, 2, HID], U8, align_bytes=64)
        nc.vector.memset(a_scales[:].rearrange("p c n -> p (c n)").bitcast(I32), 0)
        nc.vector.memset(w2_sc[:].bitcast(I32), 0)
        nc.vector.memset(wl_sc[:].rearrange("p c n -> p (c n)").bitcast(I32), 0)

        s_col = keep.tile([P, 2, 4], F32)
        nc.sync.dma_start(out=s_col[:], in_=x_scale.rearrange("o (j p m) -> p (o j) m", j=2, m=4))

        x_rows = x_bytes.rearrange("(p n) k -> p n k", n=NT)
        prior_rows = prior.rearrange("(p n) k -> p n k", n=NT)
        out_rows = out.rearrange("(p n) h -> p n h", n=NT)
        x_fp8, prior_in = [None] * PAIRS, [None] * PAIRS

        def load_x(q):
            x_fp8[q] = keep.tile([P, 2, D], U8, name="x_fp8_%d" % q)
            nc.sync.dma_start(out=x_fp8[q][:], in_=x_rows[:, 2 * q : 2 * q + 2, :])

        def load_prior(q, engine):
            prior_in[q] = keep.tile([P, 2, PRIOR], BF16, name="prior_in_%d" % q)
            engine.dma_start(out=prior_in[q][:], in_=prior_rows[:, 2 * q : 2 * q + 2, :])

        def load_scales(scale_tile, src):
            for quad in range(4):
                nc.sync.dma_start(
                    out=scale_tile[32 * quad : 32 * quad + 4, :, :].bitcast(I32),
                    in_=src[:, 4 * quad : 4 * quad + 4, :].rearrange("g q n -> q g n").bitcast(I32),
                )

        load_x(0)
        load_prior(0, nc.scalar)
        load_x(1)
        load_prior(1, nc.scalar)
        load_scales(a_scales[:, 1:3, :], wx_scales)
        wx = keep.tile([P, 2, 2 * G], U8, align_bytes=64)
        nc.sync.dma_start(out=wx[:].bitcast(I32), in_=wx_words.rearrange("g p b -> p g b").bitcast(I32))
        wp = keep.tile([P, 1, 2 * G], U8, align_bytes=64)
        nc.sync.dma_start(out=wp[:].bitcast(I32), in_=wp_words.rearrange("g p b -> p g b").bitcast(I32))
        load_scales(a_scales[:, 0:1, :], wp_scales)
        b_col = keep.tile([P, 4], BF16)
        nc.sync.dma_start(out=b_col[:], in_=b1.rearrange("(p m) -> p m", m=4))
        load_scales(w2_sc[:].rearrange("p (c n) -> p c n", c=1), w2_scales)
        load_scales(wl_sc, wl_scales)
        w2 = keep.tile([P, 1, 2 * HID], U8, align_bytes=64)
        nc.sync.dma_start(out=w2[:].bitcast(I32), in_=w2_words.rearrange("g p b -> p g b").bitcast(I32))
        load_x(2)
        wl = keep.tile([P, 2, 2 * HID], U8, align_bytes=64)
        nc.sync.dma_start(out=wl[:].bitcast(I32), in_=wl_words.rearrange("g p b -> p g b").bitcast(I32))
        load_prior(2, nc.sync)
        load_x(3)
        load_prior(3, nc.sync)

        s_all = keep.tile([P, D], F32)
        bias = keep.tile([P, 2, P, 2], F32)

        def spread_scales():
            for j in range(2):
                spread = psum.tile([P, 4, P], F32, name="spread%d" % j, tag="tr", bufs=2)
                for m in range(4):
                    nc.tensor.transpose(spread[:, m, :], s_col[:, j, m : m + 1].to_broadcast([P, P]), ident[:])
                for p0, p1 in ((0, P // 2), (P // 2, P)) if j == 0 else ((0, P),):
                    nc.scalar.activation(
                        out=s_all[:, 512 * j + 4 * p0 : 512 * j + 4 * p1].rearrange("c (p m) -> c p m", m=4),
                        in_=spread[:, :, p0:p1].rearrange("c m p -> c p m"),
                        func=ACT.Copy,
                        scale=2.0,
                    )

        def spread_bias():
            spread_b = psum.tile([P, 4, P], BF16, tag="r", bufs=1)
            for m in range(4):
                nc.tensor.transpose(spread_b[:, m, :], b_col[:, m : m + 1].to_broadcast([P, P]), ident_bf[:])
            nc.scalar.activation(
                out=bias[:], in_=spread_b[:].rearrange("c (u e) p -> c u p e", u=2), func=ACT.Copy, scale=2.0
            )

        prior_t, prior_grouped, prior_codes, prior_mx_scales = {}, {}, {}, {}

        def transpose_prior(q):
            prior_t[q] = psum.tile([P, 2, 2, P], F32, name="prior_t%d" % q, tag="h" if q == 1 else "tr", bufs=2)
            words = prior_in[q][:].rearrange("p n k -> p (n k)").bitcast(F32)
            for i in range(2):
                for u in range(2):
                    nc.tensor.transpose(prior_t[q][:, i, u, :], words[:, 256 * i + u : 256 * (i + 1) : 2], ident[:])

        def copy_prior(q):
            prior_grouped[q] = work.tile([P, 2 * P * 4], BF16, name="prior_grouped%d" % q, tag="prior_grouped", bufs=2, align_bytes=64)
            for i in range(2):
                nc.scalar.activation(
                    out=prior_grouped[q][:, 512 * i : 512 * (i + 1)].rearrange("p (r u e) -> p r u e", u=2, e=2),
                    in_=prior_t[q][:, i, :, :].rearrange("p u r -> p (u r)").bitcast(BF16).rearrange("p (u r e) -> p r u e", u=2, e=2),
                    func=ACT.Copy,
                    scale=2.0,
                )

        def quantize_prior(q):
            prior_codes[q] = keep.tile([P, 2 * P], U32, name="prior_codes%d" % q, align_bytes=64)
            prior_mx_scales[q] = keep.tile([P, 2 * P], U8, name="prior_mx_scales%d" % q, align_bytes=64)
            nc.vector.quantize_mx(out=prior_codes[q][:].bitcast(FP8X4), scales=prior_mx_scales[q][:], in_=prior_grouped[q][:])

        x_scaled, x_t, x_grouped, x_codes, x_mx_scales = {}, {}, {}, {}, {}

        def scale_x(n):
            x_scaled[n] = work.tile([P, D], BF16, name="x_scaled%d" % n, tag="x_scaled", bufs=3)
            for c0, c1 in ((0, 256), (256, 512), (512, 1024)) if n == 0 else ((0, 1024),):
                nc.vector.tensor_tensor(
                    out=x_scaled[n][:, c0:c1], in0=x_fp8[n // 2][:, n % 2, c0:c1].bitcast(FP8), in1=s_all[:, c0:c1], op=ALU.mult
                )

        def transpose_x(n):
            x_t[n] = psum.tile([P, 2, 2, P], F32, name="x_t%d" % n, tag="tr", bufs=2)
            words = x_scaled[n][:].bitcast(F32)
            for g in range(2):
                for u in range(2):
                    nc.tensor.transpose(x_t[n][:, g, u, :], words[:, 256 * g + u : 256 * (g + 1) : 2], ident[:])

        def copy_x(n):
            x_grouped[n] = work.tile([P, 2 * P * 4], BF16, name="x_grouped%d" % n, tag="x_grouped", bufs=3, align_bytes=64)
            nc.scalar.copy(
                out=x_grouped[n][:].bitcast(F32).rearrange("p (g r u) -> p g r u", g=2, u=2),
                in_=x_t[n][:].rearrange("p g u r -> p g r u"),
            )

        def quantize_x(n):
            x_codes[n] = keep.tile([P, 2 * P], U32, name="x_codes%d" % n, align_bytes=64)
            x_mx_scales[n] = keep.tile([P, 2 * P], U8, name="x_mx_scales%d" % n, align_bytes=64)
            nc.vector.quantize_mx(out=x_codes[n][:].bitcast(FP8X4), scales=x_mx_scales[n][:], in_=x_grouped[n][:])

        acc_a, r_rows, r_t, r_grouped, r_codes, r_mx_scales = {}, {}, {}, {}, {}, {}

        def matmul_a(n):
            acc_a[n] = psum.tile([P, G], F32, name="acc_a%d" % n, tag="a", bufs=1)
            c0 = P * (n % 2)
            for i in range(3):
                if i == 0:
                    codes, scales, w = prior_codes[n // 2][:, c0 : c0 + P], prior_mx_scales[n // 2][:, c0 : c0 + P], wp[:, 0, :]
                else:
                    codes, scales, w = x_codes[n][:, P * (i - 1) : P * i], x_mx_scales[n][:, P * (i - 1) : P * i], wx[:, i - 1, :]
                nc.tensor.matmul_mx(
                    out=acc_a[n][:], lhsT=codes.bitcast(FP8X4), lhsT_scale=scales, rhs=w.bitcast(FP4X4),
                    rhs_scale=a_scales[:, i, :], start=(i == 0), stop=(i == 2),
                )

        def add_bias(n):
            r_rows[n] = work.tile([P, 2, P, 2], BF16, name="r_rows%d" % n, tag="r_rows", bufs=2)
            nc.vector.tensor_tensor(
                out=r_rows[n][:], in0=acc_a[n][:].rearrange("c (p u e) -> c u p e", u=2, e=2), in1=bias[:], op=ALU.add
            )

        def transpose_r(n):
            r_t[n] = psum.tile([P, 2 * P], F32, name="r_t%d" % n, tag="r", bufs=1)
            words = r_rows[n][:].rearrange("c u p e -> c (u p e)").bitcast(F32)
            for u in range(2):
                nc.tensor.transpose(r_t[n][:, P * u : P * (u + 1)], words[:, P * u : P * (u + 1)], ident[:])

        def relu_r(n):
            r_grouped[n] = work.tile([P, P * 4], BF16, name="r_grouped%d" % n, tag="r_grouped", bufs=2, align_bytes=64)
            nc.scalar.activation(
                out=r_grouped[n][:].rearrange("p (c u e) -> p c u e", u=2, e=2),
                in_=r_t[n][:].bitcast(BF16).rearrange("p (u c e) -> p c u e", u=2, e=2),
                func=ACT.Relu,
            )

        def quantize_r(n):
            r_codes[n] = work.tile([P, P], U32, name="r_codes%d" % n, tag="r_codes", bufs=3, align_bytes=64)
            r_mx_scales[n] = work.tile([P, P], U8, name="r_mx_scales%d" % n, tag="r_mx_scales", bufs=3, align_bytes=64)
            nc.vector.quantize_mx(out=r_codes[n][:].bitcast(FP8X4), scales=r_mx_scales[n][:], in_=r_grouped[n][:])

        acc_t, acc_h, gate, res = {}, {}, {}, {}

        def matmul_t(n, j):
            acc_t[n, j] = psum.tile([P, BANK], F32, name="acc_t%d_%d" % (n, j), tag="t", bufs=2)
            nc.tensor.matmul_mx(
                out=acc_t[n, j][:], lhsT=r_codes[n][:].bitcast(FP8X4), lhsT_scale=r_mx_scales[n][:],
                rhs=w2[:, 0, 2 * BANK * j : 2 * BANK * (j + 1)].bitcast(FP4X4), rhs_scale=w2_sc[:, BANK * j : BANK * (j + 1)],
                start=True, stop=True,
            )

        def sigmoid_t(n, j):
            gate[n, j] = work.tile([P, BANK], F32, name="gate%d_%d" % (n, j), tag="gate", bufs=6)
            nc.scalar.activation(out=gate[n, j][:], in_=acc_t[n, j][:], func=ACT.Sigmoid, scale=0.5)

        def matmul_h(n, j):
            acc_h[n, j] = psum.tile([P, BANK], F32, name="acc_h%d_%d" % (n, j), tag="h", bufs=2)
            for g in range(2):
                nc.tensor.matmul_mx(
                    out=acc_h[n, j][:], lhsT=x_codes[n][:, P * g : P * (g + 1)].bitcast(FP8X4), lhsT_scale=x_mx_scales[n][:, P * g : P * (g + 1)],
                    rhs=wl[:, g, 2 * BANK * j : 2 * BANK * (j + 1)].bitcast(FP4X4), rhs_scale=wl_sc[:, g, BANK * j : BANK * (j + 1)],
                    start=(g == 0), stop=(g == 1),
                )

        def gate_and_store(n, j):
            if j == 0:
                res[n] = work.tile([P, HID], F32, name="res%d" % n, tag="res", bufs=3)
            nc.vector.scalar_tensor_tensor(
                out=res[n][:, BANK * j : BANK * (j + 1)], in0=acc_h[n, j][:], scalar=0.0, in1=gate[n, j][:], op0=ALU.max, op1=ALU.mult
            )
            if n == NT - 1:
                nc.sync.dma_start(out=out_rows[:, n, BANK * j : BANK * (j + 1)], in_=res[n][:, BANK * j : BANK * (j + 1)])
            elif j == 1:
                nc.sync.dma_start(out=out_rows[:, n, :], in_=res[n][:])

        def keep_tensor_busy(count):
            for i in range(count):
                junk = psum.tile([P, BANK], F32, name="junk", tag="t", bufs=2)
                nc.tensor.matmul(junk[:], warm[:, 0:P], warm[:], start=True, stop=True)

        def both_halves(stage, n):
            for j in range(2):
                stage(n, j)

        ctx.enter_context(tc.manual_schedule())
        keep_tensor_busy(3)
        spread_scales()
        transpose_prior(0)
        copy_prior(0)
        keep_tensor_busy(3)
        scale_x(0)
        transpose_x(0)
        copy_x(0)
        scale_x(1)
        quantize_prior(0)
        transpose_prior(1)
        transpose_x(1)
        copy_x(1)
        quantize_x(0)
        spread_bias()
        copy_prior(1)
        matmul_a(0)
        scale_x(2)
        add_bias(0)
        quantize_x(1)
        scale_x(3)
        for i in range(NT + 1):
            if i + 2 < NT:
                transpose_x(i + 2)
                copy_x(i + 2)
            if i < NT:
                transpose_r(i)
                relu_r(i)
            if i % 2 == 1 and (i + 3) // 2 < PAIRS:
                transpose_prior((i + 3) // 2)
                copy_prior((i + 3) // 2)
            if i > 0:
                both_halves(matmul_t, i - 1)
                both_halves(sigmoid_t, i - 1)
            if i + 1 < NT:
                matmul_a(i + 1)
            if i > 0:
                both_halves(matmul_h, i - 1)
            if i + 1 < NT:
                add_bias(i + 1)
            if i < NT:
                quantize_r(i)
            if i % 2 == 0 and (i + 2) // 2 < PAIRS:
                quantize_prior((i + 2) // 2)
            if i + 2 < NT:
                quantize_x(i + 2)
            if i > 0:
                both_halves(gate_and_store, i - 1)
            if i + 4 < NT:
                scale_x(i + 4)
